import numpy as np
import ml_dtypes


def mxq(x, axis, fmt="e4m3"):
    dtype, down = {"e4m3": (ml_dtypes.float8_e4m3fn, 7), "e5m2": (ml_dtypes.float8_e5m2, 14)}[fmt]
    v = np.moveaxis(np.asarray(x, np.float32).astype(ml_dtypes.bfloat16).astype(np.float64), axis, -1)
    blocks = v.reshape(v.shape[:-1] + (-1, 32))
    amax = np.abs(blocks).max(-1, keepdims=True)
    byte = np.maximum(np.where(amax > 0, np.frexp(amax)[1] - 1 + 127, 0) - down, 1)
    scale = np.exp2(byte - 127.0)
    codes = (blocks / scale).astype(np.float32).astype(dtype).astype(np.float64)
    return np.moveaxis((codes * scale).reshape(v.shape), -1, axis)


WIDE = False


def mx_kscale(k):
    if not WIDE:
        return np.ones(k)
    levels = np.array([10, -10, 5, -5, 0])
    if k % 512:
        return np.exp2(np.random.permutation(np.resize(levels, k // 32))).repeat(32)
    a = np.empty((k // 512, 16))
    for p in range(k // 512):
        a[p, :8] = np.random.permutation(np.resize(levels, 8))
        for g in range(8):
            far = levels[np.abs(levels - a[p, g]) >= 10]
            a[p, g + 8] = far[np.random.randint(len(far))]
    return np.exp2(a.ravel()).repeat(32)


def f64(x):
    return np.asarray(x).astype(np.float64)


def striped(idx):
    return np.tile(idx.reshape(-1, 16).T, (8, 1)).astype(np.uint16)


def unstriped(offs):
    return offs[:16].T.reshape(-1).astype(np.int64)


def striped8(idx):
    return np.concatenate([x.reshape(-1, 16).T for x in idx]).astype(np.uint16)


def runs(offs, k):
    lists = np.stack([offs[16 * r : 16 * r + 16].T.reshape(-1) for r in range(8)]).astype(np.int64)
    return lists[np.arange(k) % 512 // 64]


def pack_weight(w):
    k, n = w.shape
    w = f64(np.asarray(w, np.float32).astype(ml_dtypes.bfloat16)).reshape(k // 32, 32, n)
    amax = np.abs(w).max(1)
    byte = np.clip(np.where(amax > 0, np.frexp(amax)[1] - 1 + 127 - 7, 1), 1, 254)
    scaled = (w * np.exp2(127.0 - byte)[:, None, :]).reshape(k, n).astype(np.float32)
    words = np.ascontiguousarray(scaled.reshape(k // 512, 128, 4, n).transpose(0, 1, 3, 2)).astype(ml_dtypes.float8_e4m3fn).view(np.uint8)
    return words, np.ascontiguousarray(byte.astype(np.uint8).reshape(k // 512, 16, n))


def unpack_weight(words, scales):
    g, p, n, _ = words.shape
    vals = np.ascontiguousarray(words).view(ml_dtypes.float8_e4m3fn).astype(np.float64) * np.repeat(np.exp2(scales.astype(np.float64) - 127.0), 8, axis=1)[..., None]
    return vals.transpose(0, 1, 3, 2).reshape(g * 512, n)


K, T, S, H, J, G = 512, 2048, 512, 512, 512, 2048


def setup_inputs():
    n = np.random.standard_normal
    s = mx_kscale(K)[:, None]
    packed_xT = pack_weight(n((K, T)) * s)
    packed_dT = pack_weight(n((K, G)) / s)
    return {
        "x_words": packed_xT[0],
        "x_scales": packed_xT[1],
        "w1": (n((K, H)) / np.sqrt(K) / s).astype(np.float32),
        "tab": n((H, J)).astype(np.float32),
        "gs": (np.random.uniform(0.5, 1.5, (K, 1)) * s).astype(np.float32),
        "d_words": packed_dT[0],
        "d_scales": packed_dT[1],
        "offs": striped(np.random.permutation(T)[:S]),
        "n1": striped8(np.random.randint(0, J, (8, S))),
        "n2": striped8(np.stack([np.random.permutation(S) for _ in range(8)])),
        "k1": striped8(np.random.randint(0, G, (8, H))),
        "n3": striped(np.random.permutation(S)),
        "n4": striped(np.random.permutation(S)),
    }


def reference(x_words, x_scales, w1, tab, gs, d_words, d_scales, offs, n1, n2, k1, n3, n4):
    d_k1 = unpack_weight(d_words, d_scales)[np.arange(K)[:, None], runs(k1, K)]
    xq = unpack_weight(x_words, x_scales)[:, unstriped(offs)]
    y = mxq(f64(w1), 0, "e4m3").T @ xq
    z = f64(gs) * (np.abs(y - (y[np.arange(H)[:, None], runs(n2, H)]) - (f64(tab)[np.arange(H)[:, None], runs(n1, H)])))
    h = 0.0625 * ((d_k1.T @ mxq(z, 0, "e4m3")))
    return (np.tanh(h[:, unstriped(n3)] - h)) * h[:, unstriped(n4)]

@@ -1,0 +1,166 @@
+from contextlib import ExitStack
+
+import concourse.mybir as mybir
+
+F32 = mybir.dt.float32
+BF16 = mybir.dt.bfloat16
+I32 = mybir.dt.int32
+U32 = mybir.dt.uint32
+U16 = mybir.dt.uint16
+U8 = mybir.dt.uint8
+FP8X4 = mybir.dt.float8_e4m3fn_x4
+ALU = mybir.AluOpType
+ACT = mybir.ActivationFunctionType
+
+P = 128
+PACK = 4
+S = 512
+TABLE = 2048
+HALF = S // 2
+FLOPS = 2 * 2 * 512 * 512 * 512
+
+
+def tile_picked_densekinddfdif_none_p_kernel(tc, x_words, x_scales, w1, tab, gs, d_words, d_scales, offs, n1, n2, k1, n3, n4, out):
+    nc = tc.nc
+
+    def cols(u):
+        return slice(u * HALF, (u + 1) * HALF)
+
+    def entries(lst, u):
+        return lst[:, u * HALF // 16 : (u + 1) * HALF // 16]
+
+    with ExitStack() as ctx:
+        keep = ctx.enter_context(tc.tile_pool(name="keep", bufs=1))
+        psum = ctx.enter_context(tc.psum_pool(name="psum", bufs=1))
+
+        def tile(shape, dtype, name):
+            return keep.tile(shape, dtype, name=name, align_bytes=64)
+
+        lists = {name: tile([P, S // 16], U16, "list_" + name) for name in ("offs", "n1", "n2", "k1", "n3", "n4")}
+        w_raw = tile([P, PACK * S], F32, "w_raw")
+        x_tab = tile([P, TABLE], I32, "x_tab")
+        d_tab = tile([P, TABLE], I32, "d_tab")
+        xs_tab = tile([P, TABLE], U8, "xs_tab")
+        ds_tab = tile([P, TABLE], U8, "ds_tab")
+        tab_sb = [tile([P, S], F32, "tab%d" % t) for t in range(PACK)]
+        gs_sb = tile([P, PACK], F32, "gs_sb")
+
+        nc.vector.memset(xs_tab[:].bitcast(I32), 0)
+        nc.gpsimd.memset(ds_tab[:].bitcast(I32), 0)
+
+        nc.sync.dma_start(lists["offs"][:], offs)
+        nc.sync.dma_start(w_raw[:], w1.rearrange("(p j) c -> p (j c)", j=PACK))
+        for r in range(4):
+            nc.sync.dma_start(xs_tab[r:P:32, :].bitcast(I32), x_scales[0, r:16:4, :].bitcast(I32))
+        nc.sync.dma_start(x_tab[:], x_words[0].rearrange("p n t -> p (n t)").bitcast(I32))
+        nc.sync.dma_start(lists["n1"][:], n1)
+        tab_rows = tab.rearrange("(p t) c -> t p c", t=PACK)
+        for t in range(PACK):
+            nc.sync.dma_start(tab_sb[t][:], tab_rows[t])
+        nc.sync.dma_start(lists["n2"][:], n2)
+        nc.sync.dma_start(lists["k1"][:], k1)
+        for e in range(2):
+            nc.sync.dma_start(ds_tab[e:P:16, :].bitcast(I32), d_scales[0, e:16:2, :].bitcast(I32))
+        nc.sync.dma_start(d_tab[:], d_words[0].rearrange("p n t -> p (n t)").bitcast(I32))
+        nc.sync.dma_start(gs_sb[:], gs.rearrange("(p t) o -> p (t o)", t=PACK))
+        nc.sync.dma_start(lists["n3"][:], n3)
+        nc.sync.dma_start(lists["n4"][:], n4)
+
+        xs_pick = tile([P, S], U8, "xs_pick")
+        nc.vector.tensor_copy(xs_pick[:], xs_tab[:].indirect(lists["offs"][:]))
+
+        w_bf = tile([P, PACK * S], BF16, "w_bf")
+        nc.vector.tensor_copy(
+            w_bf[:].rearrange("p (t m j) -> p m j t", t=PACK, j=PACK),
+            w_raw[:].rearrange("p (j m t) -> p m j t", t=PACK, j=PACK),
+        )
+        w_codes = tile([P, S], U32, "w_codes")
+        w_scales = tile([P, S], U8, "w_scales")
+        nc.vector.quantize_mx(out=w_codes[:].bitcast(FP8X4), scales=w_scales[:], in_=w_bf[:])
+
+        x_pick = tile([P, S], U32, "x_pick")
+        banks = [psum.tile([P, S], F32, name="bank%d" % b) for b in range(8)]
+        for u in range(2):
+            nc.vector.tensor_copy(x_pick[:, cols(u)], x_tab[:].bitcast(U32).indirect(entries(lists["offs"], u)))
+            for t in range(PACK):
+                m = slice(t * P, (t + 1) * P)
+                nc.tensor.matmul_mx(
+                    out=banks[t][:, cols(u)],
+                    lhsT=w_codes[:, m].bitcast(FP8X4), lhsT_scale=w_scales[:, m],
+                    rhs=x_pick[:, cols(u)].bitcast(FP8X4), rhs_scale=xs_pick[:, cols(u)],
+                    start=True, stop=True,
+                )
+
+        tab_pick = [tile([P, S], F32, "tab_pick%d" % t) for t in range(PACK)]
+        for t in range(PACK):
+            for u in range(2):
+                nc.scalar.activation(tab_pick[t][:, cols(u)], tab_sb[t][:].indirect(entries(lists["n1"], u)), ACT.Copy)
+
+        y = [tile([P, S], F32, "y%d" % t) for t in range(PACK)]
+        for t in range(PACK):
+            nc.vector.tensor_copy(y[t][:], banks[t][:])
+
+        ds_pick = tile([P, S], U8, "ds_pick")
+        d_pick = tile([P, S], U32, "d_pick")
+        ds_plane = tile([P, S], U8, "ds_plane")
+        for u in range(2):
+            nc.vector.tensor_copy(ds_pick[:, cols(u)], ds_tab[:].indirect(entries(lists["k1"], u)))
+        nc.vector.tensor_copy(ds_plane[:].bitcast(I32), ds_pick[:].bitcast(I32))
+        for e in range(2):
+            nc.sync.dma_start(ds_plane[2 + e : P : 32, :].bitcast(I32), ds_pick[16 + e : P : 32, :].bitcast(I32))
+
+        less_tab = [tile([P, S], F32, "less_tab%d" % t) for t in range(PACK)]
+        for t in range(PACK):
+            nc.vector.tensor_tensor(less_tab[t][:], y[t][:], tab_pick[t][:], ALU.subtract)
+        for u in range(2):
+            nc.vector.tensor_copy(d_pick[:, cols(u)], d_tab[:].bitcast(U32).indirect(entries(lists["k1"], u)))
+
+        h = [tile([P, S], F32, "h%d" % b) for b in range(PACK)]
+        for u in range(2):
+            diff = tile([P, PACK * HALF], F32, "diff%d" % u)
+            for t in range(PACK):
+                y_pick = tile([P, HALF], F32, "y_pick%d%d" % (u, t))
+                nc.scalar.activation(y_pick[:], y[t][:].indirect(entries(lists["n2"], u)), ACT.Copy)
+                nc.vector.tensor_tensor(diff[:, t * HALF : (t + 1) * HALF], less_tab[t][:, cols(u)], y_pick[:], ALU.subtract)
+            size = tile([P, PACK * HALF], F32, "size%d" % u)
+            nc.scalar.activation(
+                size[:].rearrange("p (c i t) -> p c t i", t=PACK, i=4),
+                diff[:].rearrange("p (t c i) -> p c t i", t=PACK, i=4),
+                ACT.Abs,
+            )
+            z_bf = tile([P, PACK * HALF], BF16, "z_bf%d" % u)
+            nc.vector.tensor_tensor(
+                z_bf[:].rearrange("p (j t) -> p j t", t=PACK),
+                size[:].rearrange("p (j t) -> p j t", t=PACK),
+                gs_sb[:].unsqueeze(1).to_broadcast([P, HALF, PACK]),
+                ALU.mult,
+            )
+            z_codes = tile([P, HALF], U32, "z_codes%d" % u)
+            z_scales = tile([P, HALF], U8, "z_scales%d" % u)
+            nc.vector.quantize_mx(out=z_codes[:].bitcast(FP8X4), scales=z_scales[:], in_=z_bf[:])
+            for b in range(PACK):
+                m = slice(b * P, (b + 1) * P)
+                acc = banks[4 + 2 * u + b // 2][:, cols(b % 2)]
+                nc.tensor.matmul_mx(
+                    out=acc,
+                    lhsT=d_pick[:, m].bitcast(FP8X4), lhsT_scale=ds_plane[:, m],
+                    rhs=z_codes[:].bitcast(FP8X4), rhs_scale=z_scales[:],
+                    start=True, stop=True,
+                )
+            for b in range(PACK):
+                acc = banks[4 + 2 * u + b // 2][:, cols(b % 2)]
+                nc.scalar.activation(h[b][:, cols(u)], acc, ACT.Copy, scale=0.0625)
+
+        for b in range(PACK):
+            for u in range(2):
+                at3 = tile([P, HALF], F32, "at3_%d%d" % (b, u))
+                at4 = tile([P, HALF], F32, "at4_%d%d" % (b, u))
+                gap = tile([P, HALF], F32, "gap_%d%d" % (b, u))
+                bent = tile([P, HALF], F32, "bent_%d%d" % (b, u))
+                res = tile([P, HALF], F32, "res_%d%d" % (b, u))
+                nc.vector.tensor_copy(at3[:], h[b][:].indirect(entries(lists["n3"], u)))
+                nc.scalar.activation(at4[:], h[b][:].indirect(entries(lists["n4"], u)), ACT.Copy)
+                nc.vector.tensor_tensor(gap[:], at3[:], h[b][:, cols(u)], ALU.subtract)
+                nc.scalar.activation(bent[:], gap[:], ACT.Tanh)
+                nc.vector.tensor_tensor(res[:], bent[:], at4[:], ALU.mult)
+                nc.sync.dma_start(out[b * P : (b + 1) * P, cols(u)], res[:])

@@ -1,6 +1,7 @@
 from contextlib import ExitStack
 
 import concourse.mybir as mybir
+from concourse.masks import make_identity
 
 F32 = mybir.dt.float32
 BF16 = mybir.dt.bfloat16
@@ -26,8 +27,8 @@ def tile_picked_densekinddfdif_none_p_kernel(tc, x_words, x_scales, w1, tab, gs,
     def cols(u):
         return slice(u * HALF, (u + 1) * HALF)
 
-    def entries(lst, u):
-        return lst[:, u * HALF // 16 : (u + 1) * HALF // 16]
+    def entries(lst, c):
+        return lst[:, c.start // 16 : c.stop // 16]
 
     with ExitStack() as ctx:
         keep = ctx.enter_context(tc.tile_pool(name="keep", bufs=1))
@@ -37,130 +38,161 @@ def tile_picked_densekinddfdif_none_p_kernel(tc, x_words, x_scales, w1, tab, gs,
             return keep.tile(shape, dtype, name=name, align_bytes=64)
 
         lists = {name: tile([P, S // 16], U16, "list_" + name) for name in ("offs", "n1", "n2", "k1", "n3", "n4")}
-        w_raw = tile([P, PACK * S], F32, "w_raw")
+        w_raw = [tile([P, PACK * HALF], F32, "w_raw%d" % u) for u in range(2)]
         x_tab = tile([P, TABLE], I32, "x_tab")
         d_tab = tile([P, TABLE], I32, "d_tab")
         xs_tab = tile([P, TABLE], U8, "xs_tab")
         ds_tab = tile([P, TABLE], U8, "ds_tab")
         tab_sb = [tile([P, S], F32, "tab%d" % t) for t in range(PACK)]
+        h = tile([P, PACK * 2 * S], F32, "h")
+        h_blocks = h[:].rearrange("p (b j) -> p b j", b=PACK)
         gs_sb = tile([P, PACK], F32, "gs_sb")
 
         nc.vector.memset(xs_tab[:].bitcast(I32), 0)
-        nc.gpsimd.memset(ds_tab[:].bitcast(I32), 0)
+        nc.vector.memset(ds_tab[:].bitcast(I32), 0)
+        warm_in = tile([P, 1], F32, "warm_in")
+        warm_out = tile([P, 1], F32, "warm_out")
+        nc.gpsimd.memset(warm_in[:], 0.0)
+        ident = tile([P, P], F32, "ident")
+        make_identity(nc, ident[:])
+        nc.gpsimd.memset(h_blocks[:, :, S:], 0.0)
 
+        w_rows = w1.rearrange("(p j) c -> p j c", j=PACK)
         nc.sync.dma_start(lists["offs"][:], offs)
-        nc.sync.dma_start(w_raw[:], w1.rearrange("(p j) c -> p (j c)", j=PACK))
+        nc.sync.dma_start(lists["n1"][:], n1)
+        nc.sync.dma_start(gs_sb[:], gs.rearrange("(p t) o -> p (t o)", t=PACK))
+        nc.sync.dma_start(lists["k1"][:], k1)
+        nc.sync.dma_start(w_raw[0][:].rearrange("p (j c) -> p j c", j=PACK), w_rows[:, :, cols(0)])
         for r in range(4):
             nc.sync.dma_start(xs_tab[r:P:32, :].bitcast(I32), x_scales[0, r:16:4, :].bitcast(I32))
+        nc.sync.dma_start(ds_tab[0:P:8, :].bitcast(I32), d_scales[0].bitcast(I32))
+        nc.sync.dma_start(w_raw[1][:].rearrange("p (j c) -> p j c", j=PACK), w_rows[:, :, cols(1)])
         nc.sync.dma_start(x_tab[:], x_words[0].rearrange("p n t -> p (n t)").bitcast(I32))
-        nc.sync.dma_start(lists["n1"][:], n1)
+        nc.scalar.activation(warm_out[:], warm_in[:], ACT.Tanh)
         tab_rows = tab.rearrange("(p t) c -> t p c", t=PACK)
         for t in range(PACK):
             nc.sync.dma_start(tab_sb[t][:], tab_rows[t])
-        nc.sync.dma_start(lists["n2"][:], n2)
-        nc.sync.dma_start(lists["k1"][:], k1)
-        for e in range(2):
-            nc.sync.dma_start(ds_tab[e:P:16, :].bitcast(I32), d_scales[0, e:16:2, :].bitcast(I32))
+            if t == 1:
+                nc.sync.dma_start(lists["n2"][:], n2)
         nc.sync.dma_start(d_tab[:], d_words[0].rearrange("p n t -> p (n t)").bitcast(I32))
-        nc.sync.dma_start(gs_sb[:], gs.rearrange("(p t) o -> p (t o)", t=PACK))
         nc.sync.dma_start(lists["n3"][:], n3)
         nc.sync.dma_start(lists["n4"][:], n4)
 
         xs_pick = tile([P, S], U8, "xs_pick")
         nc.vector.tensor_copy(xs_pick[:], xs_tab[:].indirect(lists["offs"][:]))
 
-        w_bf = tile([P, PACK * S], BF16, "w_bf")
-        nc.vector.tensor_copy(
-            w_bf[:].rearrange("p (t m j) -> p m j t", t=PACK, j=PACK),
-            w_raw[:].rearrange("p (j m t) -> p m j t", t=PACK, j=PACK),
-        )
+        ds_pick = tile([P, S], U8, "ds_pick")
+        ds_plane = tile([P, S], U8, "ds_plane")
+        nc.vector.tensor_copy(ds_pick[:], ds_tab[:].indirect(lists["k1"][:]))
+        nc.vector.tensor_copy(ds_plane[:].bitcast(I32), ds_pick[:].bitcast(I32))
+
         w_codes = tile([P, S], U32, "w_codes")
         w_scales = tile([P, S], U8, "w_scales")
-        nc.vector.quantize_mx(out=w_codes[:].bitcast(FP8X4), scales=w_scales[:], in_=w_bf[:])
-
+        w_bf = tile([P, PACK * S], BF16, "w_bf")
+        w_dealt = w_bf[:].rearrange("p (t u m j) -> p u m j t", t=PACK, u=2, j=PACK)
+        for u in range(2):
+            nc.scalar.copy(w_dealt[:, u], w_raw[u][:].rearrange("p (j m t) -> p m j t", t=PACK, j=PACK))
         x_pick = tile([P, S], U32, "x_pick")
         banks = [psum.tile([P, S], F32, name="bank%d" % b) for b in range(8)]
         for u in range(2):
-            nc.vector.tensor_copy(x_pick[:, cols(u)], x_tab[:].bitcast(U32).indirect(entries(lists["offs"], u)))
-            for t in range(PACK):
-                m = slice(t * P, (t + 1) * P)
-                nc.tensor.matmul_mx(
-                    out=banks[t][:, cols(u)],
-                    lhsT=w_codes[:, m].bitcast(FP8X4), lhsT_scale=w_scales[:, m],
-                    rhs=x_pick[:, cols(u)].bitcast(FP8X4), rhs_scale=xs_pick[:, cols(u)],
-                    start=True, stop=True,
-                )
+            nc.vector.quantize_mx(out=w_codes[:, cols(u)].bitcast(FP8X4), scales=w_scales[:, cols(u)], in_=w_bf[:, u * 2 * S : (u + 1) * 2 * S])
+            nc.vector.tensor_copy(x_pick[:, cols(u)], x_tab[:].bitcast(U32).indirect(entries(lists["offs"], cols(u))))
+        for t, u in ((0, 0), (1, 0), (0, 1), (1, 1), (2, 0), (2, 1), (3, 0), (3, 1)):
+            m = slice(t * P, (t + 1) * P)
+            nc.tensor.matmul_mx(
+                out=banks[t][:, cols(u)],
+                lhsT=w_codes[:, m].bitcast(FP8X4), lhsT_scale=w_scales[:, m],
+                rhs=x_pick[:, cols(u)].bitcast(FP8X4), rhs_scale=xs_pick[:, cols(u)],
+                start=True, stop=True,
+            )
 
-        tab_pick = [tile([P, S], F32, "tab_pick%d" % t) for t in range(PACK)]
-        for t in range(PACK):
-            for u in range(2):
-                nc.scalar.activation(tab_pick[t][:, cols(u)], tab_sb[t][:].indirect(entries(lists["n1"], u)), ACT.Copy)
-
-        y = [tile([P, S], F32, "y%d" % t) for t in range(PACK)]
-        for t in range(PACK):
-            nc.vector.tensor_copy(y[t][:], banks[t][:])
-
-        ds_pick = tile([P, S], U8, "ds_pick")
         d_pick = tile([P, S], U32, "d_pick")
-        ds_plane = tile([P, S], U8, "ds_plane")
-        for u in range(2):
-            nc.vector.tensor_copy(ds_pick[:, cols(u)], ds_tab[:].indirect(entries(lists["k1"], u)))
-        nc.vector.tensor_copy(ds_plane[:].bitcast(I32), ds_pick[:].bitcast(I32))
-        for e in range(2):
-            nc.sync.dma_start(ds_plane[2 + e : P : 32, :].bitcast(I32), ds_pick[16 + e : P : 32, :].bitcast(I32))
 
-        less_tab = [tile([P, S], F32, "less_tab%d" % t) for t in range(PACK)]
+        def block(i):
+            return slice(i * P, (i + 1) * P)
+
+        def add_turned(plane, t, chunks, start=False, stop=False):
+            for i, c in enumerate(chunks):
+                nc.tensor.matmul(banks[4 + c][:, block(t)], lhsT=plane[:, block(i)], rhs=ident[:], is_transpose=True, start=start, stop=stop)
+
+        neg_y = [tile([P, S], F32, "neg_y%d" % t) for t in range(PACK)]
         for t in range(PACK):
-            nc.vector.tensor_tensor(less_tab[t][:], y[t][:], tab_pick[t][:], ALU.subtract)
-        for u in range(2):
-            nc.vector.tensor_copy(d_pick[:, cols(u)], d_tab[:].bitcast(U32).indirect(entries(lists["k1"], u)))
+            nc.vector.tensor_scalar(neg_y[t][:], banks[t][:], -1.0, None, ALU.mult)
 
-        h = [tile([P, S], F32, "h%d" % b) for b in range(PACK)]
-        for u in range(2):
-            diff = tile([P, PACK * HALF], F32, "diff%d" % u)
+        for t in range(2):
+            add_turned(neg_y[t], t, range(4), start=(t == 0))
+        def add_tab(u):
             for t in range(PACK):
-                y_pick = tile([P, HALF], F32, "y_pick%d%d" % (u, t))
-                nc.scalar.activation(y_pick[:], y[t][:].indirect(entries(lists["n2"], u)), ACT.Copy)
-                nc.vector.tensor_tensor(diff[:, t * HALF : (t + 1) * HALF], less_tab[t][:, cols(u)], y_pick[:], ALU.subtract)
-            size = tile([P, PACK * HALF], F32, "size%d" % u)
-            nc.scalar.activation(
-                size[:].rearrange("p (c i t) -> p c t i", t=PACK, i=4),
-                diff[:].rearrange("p (t c i) -> p c t i", t=PACK, i=4),
-                ACT.Abs,
-            )
-            z_bf = tile([P, PACK * HALF], BF16, "z_bf%d" % u)
-            nc.vector.tensor_tensor(
-                z_bf[:].rearrange("p (j t) -> p j t", t=PACK),
-                size[:].rearrange("p (j t) -> p j t", t=PACK),
-                gs_sb[:].unsqueeze(1).to_broadcast([P, HALF, PACK]),
-                ALU.mult,
-            )
-            z_codes = tile([P, HALF], U32, "z_codes%d" % u)
-            z_scales = tile([P, HALF], U8, "z_scales%d" % u)
-            nc.vector.quantize_mx(out=z_codes[:].bitcast(FP8X4), scales=z_scales[:], in_=z_bf[:])
-            for b in range(PACK):
-                m = slice(b * P, (b + 1) * P)
-                acc = banks[4 + 2 * u + b // 2][:, cols(b % 2)]
-                nc.tensor.matmul_mx(
-                    out=acc,
-                    lhsT=d_pick[:, m].bitcast(FP8X4), lhsT_scale=ds_plane[:, m],
-                    rhs=z_codes[:].bitcast(FP8X4), rhs_scale=z_scales[:],
-                    start=True, stop=True,
+                tab_pick = tile([P, HALF], F32, "tab_pick%d_%d" % (u, t))
+                window = tab_sb[t][:].indirect(entries(lists["n1"], cols(u)))
+                if t < 2 - u:
+                    nc.scalar.activation(tab_pick[:], window, ACT.Copy)
+                elif t < 2:
+                    nc.vector.tensor_copy(tab_pick[:], window)
+                else:
+                    nc.vector.tensor_tensor(tab_pick[:], window, neg_y[t][:, cols(u)], ALU.add)
+                add_turned(tab_pick, t, (2 * u, 2 * u + 1))
+
+        add_tab(0)
+        for r in range(1, 4):
+            nc.sync.dma_start(ds_plane[r:P:32, :].bitcast(I32), ds_pick[8 * r : P : 32, :].bitcast(I32))
+
+        for chunks in ((0, 1), (2,), (3,)):
+            picked = slice(chunks[0] * P, (chunks[-1] + 1) * P)
+            n = len(chunks) * P
+            for t in range(PACK):
+                y_pick = tile([P, n], F32, "y_pick%d_%d" % (chunks[0], t))[:]
+                nc.scalar.activation(y_pick, neg_y[t][:].indirect(entries(lists["n2"], picked)), ACT.Copy, scale=-1.0)
+                add_turned(y_pick, t, chunks, stop=(t == PACK - 1))
+            if chunks[0] == 0:
+                add_tab(1)
+                nc.vector.tensor_copy(d_pick[:], d_tab[:].bitcast(U32).indirect(lists["k1"][:]))
+            for c in chunks:
+                size = tile([P, S], F32, "size%d" % c)
+                for part in ((0, 1), (2, 3)) if c == 3 else ((0, 1, 2, 3),):
+                    span = slice(part[0] * P, (part[-1] + 1) * P)
+                    nc.scalar.activation(size[:, span], banks[4 + c][:, span], ACT.Abs)
+                    for t in part:
+                        nc.tensor.transpose(banks[c][:, block(t)], size[:, block(t)], ident[:])
+                z_bf = tile([P, S], BF16, "z_bf%d" % c)
+                nc.vector.tensor_tensor(
+                    z_bf[:].rearrange("p (j t) -> p j t", t=PACK),
+                    banks[c][:].rearrange("p (t j) -> p j t", t=PACK),
+                    gs_sb[:].unsqueeze(1).to_broadcast([P, P, PACK]),
+                    ALU.mult,
                 )
-            for b in range(PACK):
-                acc = banks[4 + 2 * u + b // 2][:, cols(b % 2)]
-                nc.scalar.activation(h[b][:, cols(u)], acc, ACT.Copy, scale=0.0625)
+                z_codes = tile([P, P], U32, "z_codes%d" % c)
+                z_scales = tile([P, P], U8, "z_scales%d" % c)
+                nc.vector.quantize_mx(out=z_codes[:].bitcast(FP8X4), scales=z_scales[:], in_=z_bf[:])
+                for b in range(PACK):
+                    nc.tensor.matmul_mx(
+                        out=banks[c if c == 3 and b >= 2 else 4 + c][:, block(b)],
+                        lhsT=d_pick[:, block(b)].bitcast(FP8X4), lhsT_scale=ds_plane[:, block(b)],
+                        rhs=z_codes[:].bitcast(FP8X4), rhs_scale=z_scales[:],
+                        start=True, stop=True,
+                    )
+                sums = banks[4 + c][:].rearrange("p (b j) -> p b j", j=P)
+                if c == 0:
+                    nc.vector.tensor_scalar(h_blocks[:, :, block(c)], sums, 0.0625, None, ALU.mult)
+                elif c < 3:
+                    nc.scalar.activation(h_blocks[:, :, block(c)], sums, ACT.Copy, scale=0.0625)
+                else:
+                    nc.vector.tensor_scalar(h_blocks[:, 0:2, block(c)], sums[:, 0:2, :], 0.0625, None, ALU.mult)
+                    sums = banks[c][:].rearrange("p (b j) -> p b j", j=P)
+                    nc.scalar.activation(h_blocks[:, 2:4, block(c)], sums[:, 2:4, :], ACT.Copy, scale=0.0625)
 
         for b in range(PACK):
-            for u in range(2):
-                at3 = tile([P, HALF], F32, "at3_%d%d" % (b, u))
-                at4 = tile([P, HALF], F32, "at4_%d%d" % (b, u))
-                gap = tile([P, HALF], F32, "gap_%d%d" % (b, u))
-                bent = tile([P, HALF], F32, "bent_%d%d" % (b, u))
-                res = tile([P, HALF], F32, "res_%d%d" % (b, u))
-                nc.vector.tensor_copy(at3[:], h[b][:].indirect(entries(lists["n3"], u)))
-                nc.scalar.activation(at4[:], h[b][:].indirect(entries(lists["n4"], u)), ACT.Copy)
-                nc.vector.tensor_tensor(gap[:], at3[:], h[b][:, cols(u)], ALU.subtract)
+            window = h_blocks[:, b, :]
+            for c in (cols(0), cols(1)) if b == PACK - 1 else (slice(0, S),):
+                n = c.stop - c.start
+                at3, at4, gap, bent, res = (tile([P, n], F32, "%s_%d_%d" % (nm, b, c.start)) for nm in ("at3", "at4", "gap", "bent", "res"))
+                if b == 1:
+                    nc.scalar.activation(at3[:, cols(0)], window.indirect(entries(lists["n3"], cols(0))), ACT.Copy)
+                    nc.vector.tensor_copy(at3[:, cols(1)], window.indirect(entries(lists["n3"], cols(1))))
+                else:
+                    nc.vector.tensor_copy(at3[:], window.indirect(entries(lists["n3"], c)))
+                nc.scalar.activation(at4[:], window.indirect(entries(lists["n4"], c)), ACT.Copy)
+                nc.vector.tensor_tensor(gap[:], at3[:], window[:, c], ALU.subtract)
                 nc.scalar.activation(bent[:], gap[:], ACT.Tanh)
                 nc.vector.tensor_tensor(res[:], bent[:], at4[:], ALU.mult)
-                nc.sync.dma_start(out[b * P : (b + 1) * P, cols(u)], res[:])
+                nc.sync.dma_start(out[b * P : (b + 1) * P, c], res[:])

@@ -1,7 +1,6 @@
 from contextlib import ExitStack
 
 import concourse.mybir as mybir
-from concourse.masks import make_identity
 
 F32 = mybir.dt.float32
 BF16 = mybir.dt.bfloat16
@@ -18,6 +17,7 @@ PACK = 4
 S = 512
 TABLE = 2048
 HALF = S // 2
+CHUNKS = (slice(0, 256), slice(256, 384), slice(384, 512))
 FLOPS = 2 * 2 * 512 * 512 * 512
 
 
@@ -53,8 +53,6 @@ def tile_picked_densekinddfdif_none_p_kernel(tc, x_words, x_scales, w1, tab, gs,
         warm_in = tile([P, 1], F32, "warm_in")
         warm_out = tile([P, 1], F32, "warm_out")
         nc.gpsimd.memset(warm_in[:], 0.0)
-        ident = tile([P, P], F32, "ident")
-        make_identity(nc, ident[:])
         nc.gpsimd.memset(h_blocks[:, :, S:], 0.0)
 
         w_rows = w1.rearrange("(p j) c -> p j c", j=PACK)
@@ -77,6 +75,13 @@ def tile_picked_densekinddfdif_none_p_kernel(tc, x_words, x_scales, w1, tab, gs,
         nc.sync.dma_start(d_tab[:], d_words[0].rearrange("p n t -> p (n t)").bitcast(I32))
         nc.sync.dma_start(lists["n3"][:], n3)
         nc.sync.dma_start(lists["n4"][:], n4)
+
+        gs_sign = tile([P, PACK * HALF], BF16, "gs_sign")
+        nc.scalar.activation(
+            gs_sign[:].rearrange("p (j t) -> p j t", t=PACK),
+            gs_sb[:].unsqueeze(1).to_broadcast([P, HALF, PACK]),
+            ACT.Sign,
+        )
 
         xs_pick = tile([P, S], U8, "xs_pick")
         nc.vector.tensor_copy(xs_pick[:], xs_tab[:].indirect(lists["offs"][:]))
@@ -111,75 +116,70 @@ def tile_picked_densekinddfdif_none_p_kernel(tc, x_words, x_scales, w1, tab, gs,
         def block(i):
             return slice(i * P, (i + 1) * P)
 
-        def add_turned(plane, t, chunks, start=False, stop=False):
-            for i, c in enumerate(chunks):
-                nc.tensor.matmul(banks[4 + c][:, block(t)], lhsT=plane[:, block(i)], rhs=ident[:], is_transpose=True, start=start, stop=stop)
-
-        neg_y = [tile([P, S], F32, "neg_y%d" % t) for t in range(PACK)]
+        y = [tile([P, S], F32, "y%d" % t) for t in range(PACK)]
         for t in range(PACK):
-            nc.vector.tensor_scalar(neg_y[t][:], banks[t][:], -1.0, None, ALU.mult)
+            nc.scalar.activation(y[t][:], banks[t][:], ACT.Copy, scale=gs_sb[:, t : t + 1])
 
-        for t in range(2):
-            add_turned(neg_y[t], t, range(4), start=(t == 0))
-        def add_tab(u):
+        tab_less_y = [tile([P, PACK * HALF], F32, "tab_less_y%d" % u) for u in range(2)]
+
+        def make_tab_less_y(u):
             for t in range(PACK):
                 tab_pick = tile([P, HALF], F32, "tab_pick%d_%d" % (u, t))
                 window = tab_sb[t][:].indirect(entries(lists["n1"], cols(u)))
-                if t < 2 - u:
+                if t == 0:
                     nc.scalar.activation(tab_pick[:], window, ACT.Copy)
-                elif t < 2:
-                    nc.vector.tensor_copy(tab_pick[:], window)
                 else:
-                    nc.vector.tensor_tensor(tab_pick[:], window, neg_y[t][:, cols(u)], ALU.add)
-                add_turned(tab_pick, t, (2 * u, 2 * u + 1))
+                    nc.vector.tensor_copy(tab_pick[:], window)
+                nc.vector.scalar_tensor_tensor(
+                    tab_less_y[u][:, t * HALF : (t + 1) * HALF], tab_pick[:], gs_sb[:, t : t + 1], y[t][:, cols(u)], ALU.mult, ALU.subtract
+                )
 
-        add_tab(0)
+        make_tab_less_y(0)
         for r in range(1, 4):
             nc.sync.dma_start(ds_plane[r:P:32, :].bitcast(I32), ds_pick[8 * r : P : 32, :].bitcast(I32))
 
-        for chunks in ((0, 1), (2,), (3,)):
-            picked = slice(chunks[0] * P, (chunks[-1] + 1) * P)
-            n = len(chunks) * P
+        for c in CHUNKS:
+            n = c.stop - c.start
+            y_pick = tile([P, PACK * n], F32, "y_pick%d" % c.start)
+            diff = tile([P, PACK * n], F32, "diff%d" % c.start)
             for t in range(PACK):
-                y_pick = tile([P, n], F32, "y_pick%d_%d" % (chunks[0], t))[:]
-                nc.scalar.activation(y_pick, neg_y[t][:].indirect(entries(lists["n2"], picked)), ACT.Copy, scale=-1.0)
-                add_turned(y_pick, t, chunks, stop=(t == PACK - 1))
-            if chunks[0] == 0:
-                add_tab(1)
-                nc.vector.tensor_copy(d_pick[:], d_tab[:].bitcast(U32).indirect(lists["k1"][:]))
-            for c in chunks:
-                size = tile([P, S], F32, "size%d" % c)
-                for part in ((0, 1), (2, 3)) if c == 3 else ((0, 1, 2, 3),):
-                    span = slice(part[0] * P, (part[-1] + 1) * P)
-                    nc.scalar.activation(size[:, span], banks[4 + c][:, span], ACT.Abs)
-                    for t in part:
-                        nc.tensor.transpose(banks[c][:, block(t)], size[:, block(t)], ident[:])
-                z_bf = tile([P, S], BF16, "z_bf%d" % c)
+                nc.scalar.activation(y_pick[:, t * n : (t + 1) * n], y[t][:].indirect(entries(lists["n2"], c)), ACT.Copy)
+            less_planes = tab_less_y[c.start // HALF][:].rearrange("p (t j) -> p t j", t=PACK)[:, :, c.start % HALF : c.start % HALF + n]
+            for ts in (slice(0, 3), slice(3, 4)):
                 nc.vector.tensor_tensor(
-                    z_bf[:].rearrange("p (j t) -> p j t", t=PACK),
-                    banks[c][:].rearrange("p (t j) -> p j t", t=PACK),
-                    gs_sb[:].unsqueeze(1).to_broadcast([P, P, PACK]),
-                    ALU.mult,
+                    diff[:].rearrange("p (t j) -> p t j", t=PACK)[:, ts, :],
+                    less_planes[:, ts, :],
+                    y_pick[:].rearrange("p (t j) -> p t j", t=PACK)[:, ts, :],
+                    ALU.add,
                 )
-                z_codes = tile([P, P], U32, "z_codes%d" % c)
-                z_scales = tile([P, P], U8, "z_scales%d" % c)
-                nc.vector.quantize_mx(out=z_codes[:].bitcast(FP8X4), scales=z_scales[:], in_=z_bf[:])
-                for b in range(PACK):
+            if c.start == 0:
+                make_tab_less_y(1)
+                nc.vector.tensor_copy(d_pick[:], d_tab[:].bitcast(U32).indirect(lists["k1"][:]))
+            size = tile([P, PACK * n], BF16, "size%d" % c.start)
+            nc.scalar.activation(
+                size[:].rearrange("p (c i t) -> p c t i", t=PACK, i=4),
+                diff[:].rearrange("p (t c i) -> p c t i", t=PACK, i=4),
+                ACT.Abs,
+            )
+            z_bf = tile([P, PACK * n], BF16, "z_bf%d" % c.start)
+            nc.vector.tensor_tensor(z_bf[:], size[:], gs_sign[:, : PACK * n], ALU.mult)
+            z_codes = tile([P, n], U32, "z_codes%d" % c.start)
+            z_scales = tile([P, n], U8, "z_scales%d" % c.start)
+            nc.vector.quantize_mx(out=z_codes[:].bitcast(FP8X4), scales=z_scales[:], in_=z_bf[:])
+            for g in range(2):
+                bank = banks[(4 + 2 * CHUNKS.index(c) + g) % 8][:, : 2 * n]
+                for b in range(2):
                     nc.tensor.matmul_mx(
-                        out=banks[c if c == 3 and b >= 2 else 4 + c][:, block(b)],
-                        lhsT=d_pick[:, block(b)].bitcast(FP8X4), lhsT_scale=ds_plane[:, block(b)],
+                        out=bank[:, b * n : (b + 1) * n],
+                        lhsT=d_pick[:, block(2 * g + b)].bitcast(FP8X4), lhsT_scale=ds_plane[:, block(2 * g + b)],
                         rhs=z_codes[:].bitcast(FP8X4), rhs_scale=z_scales[:],
                         start=True, stop=True,
                     )
-                sums = banks[4 + c][:].rearrange("p (b j) -> p b j", j=P)
-                if c == 0:
-                    nc.vector.tensor_scalar(h_blocks[:, :, block(c)], sums, 0.0625, None, ALU.mult)
-                elif c < 3:
-                    nc.scalar.activation(h_blocks[:, :, block(c)], sums, ACT.Copy, scale=0.0625)
+                sums = bank.rearrange("p (b j) -> p b j", b=2)
+                if c.stop == S and g == 0:
+                    nc.vector.tensor_scalar(h_blocks[:, 0:2, c], sums, 0.0625, None, ALU.mult)
                 else:
-                    nc.vector.tensor_scalar(h_blocks[:, 0:2, block(c)], sums[:, 0:2, :], 0.0625, None, ALU.mult)
-                    sums = banks[c][:].rearrange("p (b j) -> p b j", j=P)
-                    nc.scalar.activation(h_blocks[:, 2:4, block(c)], sums[:, 2:4, :], ACT.Copy, scale=0.0625)
+                    nc.scalar.activation(h_blocks[:, 2 * g : 2 * g + 2, c], sums, ACT.Copy, scale=0.0625)
 
         for b in range(PACK):
             window = h_blocks[:, b, :]

@@ -44,7 +44,7 @@ def tile_picked_densekinddfdif_none_p_kernel(tc, x_words, x_scales, w1, tab, gs,
         xs_tab = tile([P, TABLE], U8, "xs_tab")
         ds_tab = tile([P, TABLE], U8, "ds_tab")
         tab_sb = [tile([P, S], F32, "tab%d" % t) for t in range(PACK)]
-        h = tile([P, PACK * 2 * S], F32, "h")
+        h = tile([P, PACK * S], F32, "h")
         h_blocks = h[:].rearrange("p (b j) -> p b j", b=PACK)
         gs_sb = tile([P, PACK], F32, "gs_sb")
 
@@ -53,7 +53,6 @@ def tile_picked_densekinddfdif_none_p_kernel(tc, x_words, x_scales, w1, tab, gs,
         warm_in = tile([P, 1], F32, "warm_in")
         warm_out = tile([P, 1], F32, "warm_out")
         nc.gpsimd.memset(warm_in[:], 0.0)
-        nc.gpsimd.memset(h_blocks[:, :, S:], 0.0)
 
         w_rows = w1.rearrange("(p j) c -> p j c", j=PACK)
         nc.sync.dma_start(lists["offs"][:], offs)
@@ -176,19 +175,20 @@ def tile_picked_densekinddfdif_none_p_kernel(tc, x_words, x_scales, w1, tab, gs,
                         start=True, stop=True,
                     )
                 sums = bank.rearrange("p (b j) -> p b j", b=2)
-                if c.stop == S and g == 0:
+                if c.start > 0 and g == 0:
                     nc.vector.tensor_scalar(h_blocks[:, 0:2, c], sums, 0.0625, None, ALU.mult)
                 else:
                     nc.scalar.activation(h_blocks[:, 2 * g : 2 * g + 2, c], sums, ACT.Copy, scale=0.0625)
 
         for b in range(PACK):
-            window = h_blocks[:, b, :]
+            window = h[:, b * S : min(b + 2, PACK) * S]
             for c in (cols(0), cols(1)) if b == PACK - 1 else (slice(0, S),):
                 n = c.stop - c.start
                 at3, at4, gap, bent, res = (tile([P, n], F32, "%s_%d_%d" % (nm, b, c.start)) for nm in ("at3", "at4", "gap", "bent", "res"))
                 if b == 1:
-                    nc.scalar.activation(at3[:, cols(0)], window.indirect(entries(lists["n3"], cols(0))), ACT.Copy)
-                    nc.vector.tensor_copy(at3[:, cols(1)], window.indirect(entries(lists["n3"], cols(1))))
+                    first, second = slice(0, 384), slice(384, S)
+                    nc.scalar.activation(at3[:, first], window.indirect(entries(lists["n3"], first)), ACT.Copy)
+                    nc.vector.tensor_copy(at3[:, second], window.indirect(entries(lists["n3"], second)))
                 else:
                     nc.vector.tensor_copy(at3[:], window.indirect(entries(lists["n3"], c)))
                 nc.scalar.activation(at4[:], window.indirect(entries(lists["n4"], c)), ACT.Copy)

@@ -44,7 +44,7 @@ def tile_picked_densekinddfdif_none_p_kernel(tc, x_words, x_scales, w1, tab, gs,
         xs_tab = tile([P, TABLE], U8, "xs_tab")
         ds_tab = tile([P, TABLE], U8, "ds_tab")
         tab_sb = [tile([P, S], F32, "tab%d" % t) for t in range(PACK)]
-        h = tile([P, PACK * S], F32, "h")
+        h = tile([P, PACK * 2 * S], F32, "h")
         h_blocks = h[:].rearrange("p (b j) -> p b j", b=PACK)
         gs_sb = tile([P, PACK], F32, "gs_sb")
 
@@ -53,6 +53,7 @@ def tile_picked_densekinddfdif_none_p_kernel(tc, x_words, x_scales, w1, tab, gs,
         warm_in = tile([P, 1], F32, "warm_in")
         warm_out = tile([P, 1], F32, "warm_out")
         nc.gpsimd.memset(warm_in[:], 0.0)
+        nc.vector.memset(h_blocks[:, :, S:], 0.0)
 
         w_rows = w1.rearrange("(p j) c -> p j c", j=PACK)
         nc.sync.dma_start(lists["offs"][:], offs)
@@ -181,7 +182,7 @@ def tile_picked_densekinddfdif_none_p_kernel(tc, x_words, x_scales, w1, tab, gs,
                     nc.scalar.activation(h_blocks[:, 2 * g : 2 * g + 2, c], sums, ACT.Copy, scale=0.0625)
 
         for b in range(PACK):
-            window = h[:, b * S : min(b + 2, PACK) * S]
+            window = h_blocks[:, b, :]
             for c in (cols(0), cols(1)) if b == PACK - 1 else (slice(0, S),):
                 n = c.stop - c.start
                 at3, at4, gap, bent, res = (tile([P, n], F32, "%s_%d_%d" % (nm, b, c.start)) for nm in ("at3", "at4", "gap", "bent", "res"))

from contextlib import ExitStack

import concourse.mybir as mybir

F32 = mybir.dt.float32
BF16 = mybir.dt.bfloat16
I32 = mybir.dt.int32
U32 = mybir.dt.uint32
U16 = mybir.dt.uint16
U8 = mybir.dt.uint8
FP8X4 = mybir.dt.float8_e4m3fn_x4
ALU = mybir.AluOpType
ACT = mybir.ActivationFunctionType

P = 128
PACK = 4
S = 512
TABLE = 2048
HALF = S // 2
CHUNKS = (slice(0, 256), slice(256, 384), slice(384, 512))
FLOPS = 2 * 2 * 512 * 512 * 512


def tile_picked_densekinddfdif_none_p_kernel(tc, x_words, x_scales, w1, tab, gs, d_words, d_scales, offs, n1, n2, k1, n3, n4, out):
    nc = tc.nc

    def cols(u):
        return slice(u * HALF, (u + 1) * HALF)

    def entries(lst, c):
        return lst[:, c.start // 16 : c.stop // 16]

    with ExitStack() as ctx:
        keep = ctx.enter_context(tc.tile_pool(name="keep", bufs=1))
        psum = ctx.enter_context(tc.psum_pool(name="psum", bufs=1))

        def tile(shape, dtype, name):
            return keep.tile(shape, dtype, name=name, align_bytes=64)

        lists = {name: tile([P, S // 16], U16, "list_" + name) for name in ("offs", "n1", "n2", "k1", "n3", "n4")}
        w_raw = [tile([P, PACK * HALF], F32, "w_raw%d" % u) for u in range(2)]
        x_tab = tile([P, TABLE], I32, "x_tab")
        d_tab = tile([P, TABLE], I32, "d_tab")
        xs_tab = tile([P, TABLE], U8, "xs_tab")
        ds_tab = tile([P, TABLE], U8, "ds_tab")
        tab_sb = [tile([P, S], F32, "tab%d" % t) for t in range(PACK)]
        h = tile([P, PACK * 2 * S], F32, "h")
        h_blocks = h[:].rearrange("p (b j) -> p b j", b=PACK)
        gs_sb = tile([P, PACK], F32, "gs_sb")

        nc.vector.memset(xs_tab[:].bitcast(I32), 0)
        nc.vector.memset(ds_tab[:].bitcast(I32), 0)
        warm_in = tile([P, 1], F32, "warm_in")
        warm_out = tile([P, 1], F32, "warm_out")
        nc.gpsimd.memset(warm_in[:], 0.0)
        nc.vector.memset(h_blocks[:, :, S:], 0.0)

        w_rows = w1.rearrange("(p j) c -> p j c", j=PACK)
        nc.sync.dma_start(lists["offs"][:], offs)
        nc.sync.dma_start(lists["n1"][:], n1)
        nc.sync.dma_start(gs_sb[:], gs.rearrange("(p t) o -> p (t o)", t=PACK))
        nc.sync.dma_start(lists["k1"][:], k1)
        nc.sync.dma_start(w_raw[0][:].rearrange("p (j c) -> p j c", j=PACK), w_rows[:, :, cols(0)])
        for r in range(4):
            nc.sync.dma_start(xs_tab[r:P:32, :].bitcast(I32), x_scales[0, r:16:4, :].bitcast(I32))
        nc.sync.dma_start(ds_tab[0:P:8, :].bitcast(I32), d_scales[0].bitcast(I32))
        nc.sync.dma_start(w_raw[1][:].rearrange("p (j c) -> p j c", j=PACK), w_rows[:, :, cols(1)])
        nc.sync.dma_start(x_tab[:], x_words[0].rearrange("p n t -> p (n t)").bitcast(I32))
        nc.scalar.activation(warm_out[:], warm_in[:], ACT.Tanh)
        tab_rows = tab.rearrange("(p t) c -> t p c", t=PACK)
        for t in range(PACK):
            nc.sync.dma_start(tab_sb[t][:], tab_rows[t])
            if t == 1:
                nc.sync.dma_start(lists["n2"][:], n2)
        nc.sync.dma_start(d_tab[:], d_words[0].rearrange("p n t -> p (n t)").bitcast(I32))
        nc.sync.dma_start(lists["n3"][:], n3)
        nc.sync.dma_start(lists["n4"][:], n4)

        gs_sign = tile([P, PACK * HALF], BF16, "gs_sign")
        nc.scalar.activation(
            gs_sign[:].rearrange("p (j t) -> p j t", t=PACK),
            gs_sb[:].unsqueeze(1).to_broadcast([P, HALF, PACK]),
            ACT.Sign,
        )

        xs_pick = tile([P, S], U8, "xs_pick")
        nc.vector.tensor_copy(xs_pick[:], xs_tab[:].indirect(lists["offs"][:]))

        ds_pick = tile([P, S], U8, "ds_pick")
        ds_plane = tile([P, S], U8, "ds_plane")
        nc.vector.tensor_copy(ds_pick[:], ds_tab[:].indirect(lists["k1"][:]))
        nc.vector.tensor_copy(ds_plane[:].bitcast(I32), ds_pick[:].bitcast(I32))

        w_codes = tile([P, S], U32, "w_codes")
        w_scales = tile([P, S], U8, "w_scales")
        w_bf = tile([P, PACK * S], BF16, "w_bf")
        w_dealt = w_bf[:].rearrange("p (t u m j) -> p u m j t", t=PACK, u=2, j=PACK)
        for u in range(2):
            nc.scalar.copy(w_dealt[:, u], w_raw[u][:].rearrange("p (j m t) -> p m j t", t=PACK, j=PACK))
        x_pick = tile([P, S], U32, "x_pick")
        banks = [psum.tile([P, S], F32, name="bank%d" % b) for b in range(8)]
        for u in range(2):
            nc.vector.quantize_mx(out=w_codes[:, cols(u)].bitcast(FP8X4), scales=w_scales[:, cols(u)], in_=w_bf[:, u * 2 * S : (u + 1) * 2 * S])
            nc.vector.tensor_copy(x_pick[:, cols(u)], x_tab[:].bitcast(U32).indirect(entries(lists["offs"], cols(u))))
        for t, u in ((0, 0), (1, 0), (0, 1), (1, 1), (2, 0), (2, 1), (3, 0), (3, 1)):
            m = slice(t * P, (t + 1) * P)
            nc.tensor.matmul_mx(
                out=banks[t][:, cols(u)],
                lhsT=w_codes[:, m].bitcast(FP8X4), lhsT_scale=w_scales[:, m],
                rhs=x_pick[:, cols(u)].bitcast(FP8X4), rhs_scale=xs_pick[:, cols(u)],
                start=True, stop=True,
            )

        d_pick = tile([P, S], U32, "d_pick")

        def block(i):
            return slice(i * P, (i + 1) * P)

        y = [tile([P, S], F32, "y%d" % t) for t in range(PACK)]
        for t in range(PACK):
            nc.scalar.activation(y[t][:], banks[t][:], ACT.Copy, scale=gs_sb[:, t : t + 1])

        tab_less_y = [tile([P, PACK * HALF], F32, "tab_less_y%d" % u) for u in range(2)]

        def make_tab_less_y(u):
            for t in range(PACK):
                tab_pick = tile([P, HALF], F32, "tab_pick%d_%d" % (u, t))
                window = tab_sb[t][:].indirect(entries(lists["n1"], cols(u)))
                if t == 0:
                    nc.scalar.activation(tab_pick[:], window, ACT.Copy)
                else:
                    nc.vector.tensor_copy(tab_pick[:], window)
                nc.vector.scalar_tensor_tensor(
                    tab_less_y[u][:, t * HALF : (t + 1) * HALF], tab_pick[:], gs_sb[:, t : t + 1], y[t][:, cols(u)], ALU.mult, ALU.subtract
                )

        make_tab_less_y(0)
        for r in range(1, 4):
            nc.sync.dma_start(ds_plane[r:P:32, :].bitcast(I32), ds_pick[8 * r : P : 32, :].bitcast(I32))

        for c in CHUNKS:
            n = c.stop - c.start
            y_pick = tile([P, PACK * n], F32, "y_pick%d" % c.start)
            diff = tile([P, PACK * n], F32, "diff%d" % c.start)
            for t in range(PACK):
                nc.scalar.activation(y_pick[:, t * n : (t + 1) * n], y[t][:].indirect(entries(lists["n2"], c)), ACT.Copy)
            less_planes = tab_less_y[c.start // HALF][:].rearrange("p (t j) -> p t j", t=PACK)[:, :, c.start % HALF : c.start % HALF + n]
            for ts in (slice(0, 3), slice(3, 4)):
                nc.vector.tensor_tensor(
                    diff[:].rearrange("p (t j) -> p t j", t=PACK)[:, ts, :],
                    less_planes[:, ts, :],
                    y_pick[:].rearrange("p (t j) -> p t j", t=PACK)[:, ts, :],
                    ALU.add,
                )
            if c.start == 0:
                make_tab_less_y(1)
                nc.vector.tensor_copy(d_pick[:], d_tab[:].bitcast(U32).indirect(lists["k1"][:]))
            size = tile([P, PACK * n], BF16, "size%d" % c.start)
            nc.scalar.activation(
                size[:].rearrange("p (c i t) -> p c t i", t=PACK, i=4),
                diff[:].rearrange("p (t c i) -> p c t i", t=PACK, i=4),
                ACT.Abs,
            )
            z_bf = tile([P, PACK * n], BF16, "z_bf%d" % c.start)
            nc.vector.tensor_tensor(z_bf[:], size[:], gs_sign[:, : PACK * n], ALU.mult)
            z_codes = tile([P, n], U32, "z_codes%d" % c.start)
            z_scales = tile([P, n], U8, "z_scales%d" % c.start)
            nc.vector.quantize_mx(out=z_codes[:].bitcast(FP8X4), scales=z_scales[:], in_=z_bf[:])
            for g in range(2):
                bank = banks[(4 + 2 * CHUNKS.index(c) + g) % 8][:, : 2 * n]
                for b in range(2):
                    nc.tensor.matmul_mx(
                        out=bank[:, b * n : (b + 1) * n],
                        lhsT=d_pick[:, block(2 * g + b)].bitcast(FP8X4), lhsT_scale=ds_plane[:, block(2 * g + b)],
                        rhs=z_codes[:].bitcast(FP8X4), rhs_scale=z_scales[:],
                        start=True, stop=True,
                    )
                sums = bank.rearrange("p (b j) -> p b j", b=2)
                if c.start > 0 and g == 0:
                    nc.vector.tensor_scalar(h_blocks[:, 0:2, c], sums, 0.0625, None, ALU.mult)
                else:
                    nc.scalar.activation(h_blocks[:, 2 * g : 2 * g + 2, c], sums, ACT.Copy, scale=0.0625)

        for b in range(PACK):
            window = h_blocks[:, b, :]
            for c in (cols(0), cols(1)) if b == PACK - 1 else (slice(0, S),):
                n = c.stop - c.start
                at3, at4, gap, bent, res = (tile([P, n], F32, "%s_%d_%d" % (nm, b, c.start)) for nm in ("at3", "at4", "gap", "bent", "res"))
                if b == 1:
                    first, second = slice(0, 384), slice(384, S)
                    nc.scalar.activation(at3[:, first], window.indirect(entries(lists["n3"], first)), ACT.Copy)
                    nc.vector.tensor_copy(at3[:, second], window.indirect(entries(lists["n3"], second)))
                else:
                    nc.vector.tensor_copy(at3[:], window.indirect(entries(lists["n3"], c)))
                nc.scalar.activation(at4[:], window.indirect(entries(lists["n4"], c)), ACT.Copy)
                nc.vector.tensor_tensor(gap[:], at3[:], window[:, c], ALU.subtract)
                nc.scalar.activation(bent[:], gap[:], ACT.Tanh)
                nc.vector.tensor_tensor(res[:], bent[:], at4[:], ALU.mult)
                nc.sync.dma_start(out[b * P : (b + 1) * P, c], res[:])
